import numpy as np
import ml_dtypes


def mxq(x, axis, fmt="e4m3"):
    dtype, down = {"e4m3": (ml_dtypes.float8_e4m3fn, 7), "e5m2": (ml_dtypes.float8_e5m2, 14)}[fmt]
    v = np.moveaxis(np.asarray(x, np.float32).astype(ml_dtypes.bfloat16).astype(np.float64), axis, -1)
    blocks = v.reshape(v.shape[:-1] + (-1, 32))
    amax = np.abs(blocks).max(-1, keepdims=True)
    byte = np.maximum(np.where(amax > 0, np.frexp(amax)[1] - 1 + 127, 0) - down, 1)
    scale = np.exp2(byte - 127.0)
    codes = (blocks / scale).astype(np.float32).astype(dtype).astype(np.float64)
    return np.moveaxis((codes * scale).reshape(v.shape), -1, axis)


WIDE = False


def mx_kscale(k):
    if not WIDE:
        return np.ones(k)
    levels = np.array([10, -10, 5, -5, 0])
    if k % 512:
        return np.exp2(np.random.permutation(np.resize(levels, k // 32))).repeat(32)
    a = np.empty((k // 512, 16))
    for p in range(k // 512):
        a[p, :8] = np.random.permutation(np.resize(levels, 8))
        for g in range(8):
            far = levels[np.abs(levels - a[p, g]) >= 10]
            a[p, g + 8] = far[np.random.randint(len(far))]
    return np.exp2(a.ravel()).repeat(32)


def f64(x):
    return np.asarray(x).astype(np.float64)


def striped8(idx):
    return np.asarray(idx).reshape(8, -1, 16).transpose(0, 2, 1).reshape(128, -1).astype(np.uint16)


def unstriped8(offs):
    return offs.reshape(8, 16, -1).transpose(0, 2, 1).reshape(8, -1).astype(np.int64)


def pick8(x, idx, run):
    r = np.arange(len(x))
    return x[r[:, None], idx[r % (8 * run) // run]]


E2M1 = np.array([0.0, 0.5, 1.0, 1.5, 2.0, 3.0, 4.0, 6.0, -0.0, -0.5, -1.0, -1.5, -2.0, -3.0, -4.0, -6.0])


def pack_weight(w, fmt):
    k, n = w.shape
    w = f64(np.asarray(w, np.float32).astype(ml_dtypes.bfloat16)).reshape(k // 32, 32, n)
    amax = np.abs(w).max(1)
    if fmt == "e4m3":
        byte = np.frexp(amax)[1] - 1 + 127 - 7
    else:
        mant, ex = np.frexp(amax / 6.0)
        byte = np.where(mant > 0.5, ex, ex - 1) + 127
    byte = np.clip(np.where(amax > 0, byte, 1), 1, 254)
    scaled = (w * np.exp2(127.0 - byte)[:, None, :]).reshape(k, n).astype(np.float32)
    by_word = np.ascontiguousarray(scaled.reshape(k // 512, 128, 4, n).transpose(0, 1, 3, 2))
    if fmt == "e4m3":
        words = by_word.astype(ml_dtypes.float8_e4m3fn).view(np.uint8)
    else:
        c = by_word.astype(ml_dtypes.float4_e2m1fn).view(np.uint8) & 0xF
        words = (c[..., 0::2] | (c[..., 1::2] << 4)).reshape(k // 512, 128, 2 * n)
    return np.ascontiguousarray(words), np.ascontiguousarray(byte.astype(np.uint8).reshape(k // 512, 16, n))


def unpack_weight(words, scales, fmt):
    g, _, n = scales.shape
    words = np.ascontiguousarray(words).reshape(g, 128, n, -1)
    if fmt == "e4m3":
        vals = words.view(ml_dtypes.float8_e4m3fn).astype(np.float64)
    else:
        nib = np.empty((g, 128, n, 4), np.uint8)
        nib[..., 0::2] = words & 0xF
        nib[..., 1::2] = words >> 4
        vals = E2M1[nib]
    vals = vals * np.repeat(np.exp2(scales.astype(np.float64) - 127.0), 8, axis=1)[..., None]
    return vals.transpose(0, 1, 3, 2).reshape(g * 512, n)


D, K, T, U, I, Q = 512, 512, 1024, 1024, 512, 128


def setup_inputs():
    n = np.random.standard_normal
    idx = np.stack([np.random.permutation(T)[:I] for _ in range(8)])
    idx2 = np.stack([np.random.permutation(U)[:I] for _ in range(8)])
    idx3 = np.stack([np.random.permutation(U)[:I] for _ in range(8)])
    idx4 = np.stack([np.random.permutation(T)[:I] for _ in range(8)])
    fd = mx_kscale(D)
    fk = mx_kscale(K)
    wqp = pack_weight(n((D, K)) * 1.0 / np.sqrt(D) * fd[:, None] * fk, "e4m3")
    cachep = pack_weight(n((K, T)) * 1.0 / np.sqrt(K) / fk[:, None], "e2m1")
    draftp = pack_weight(n((D, U)) * 1.0 / np.sqrt(D) * fd[:, None], "e4m3")
    return {
        "states": (n((D, Q)) * 0.95 / fd[:, None]).astype(np.float32),
        "wq_words": wqp[0],
        "wq_scales": wqp[1],
        "cache_words": cachep[0],
        "cache_scales": cachep[1],
        "draft_words": draftp[0],
        "draft_scales": draftp[1],
        "offs": striped8(idx),
        "offs2": striped8(idx2),
        "offs3": striped8(idx3),
        "offs4": striped8(idx4),
    }


def reference(states, wq_words, wq_scales, cache_words, cache_scales, draft_words, draft_scales, offs, offs2, offs3, offs4):
    idx = unstriped8(offs)
    idx2 = unstriped8(offs2)
    idx3 = unstriped8(offs3)
    idx4 = unstriped8(offs4)
    wqu = unpack_weight(wq_words, wq_scales, "e4m3")
    cacheu = unpack_weight(cache_words, cache_scales, "e2m1")
    draftu = unpack_weight(draft_words, draft_scales, "e4m3")
    statesq = mxq(f64(states), 0, "e4m3")
    qv = wqu.T @ statesq
    qvq = mxq(qv, 0, "e4m3")
    a = qvq.T @ cacheu
    b = statesq.T @ draftu
    a1 = np.pad(a, ((0, 0), (1, 0)))[:, :T]
    dl = a - a1
    f1 = np.zeros((Q, U))
    f1[np.arange(Q)[:, None], idx2[np.arange(Q) % 128 // 16]] = pick8(dl, idx, 16)
    bb = b + f1
    v = np.maximum(pick8(bb, idx3, 16), pick8(dl, idx4, 16))
    f2 = np.zeros((Q, T))
    f2[np.arange(Q)[:, None], idx[np.arange(Q) % 128 // 16]] = v
    aa = a - f2
    y = pick8(aa, idx4, 16)
    return y

@@ -1,0 +1,172 @@
+from contextlib import ExitStack
+
+import concourse.mybir as mybir
+
+D, K, T, U, I, Q = 512, 512, 1024, 1024, 512, 128
+FLOPS = 2 * (D * K * Q + K * T * Q + D * U * Q)
+
+F32 = mybir.dt.float32
+BF16 = mybir.dt.bfloat16
+I32 = mybir.dt.int32
+U32 = mybir.dt.uint32
+U16 = mybir.dt.uint16
+U8 = mybir.dt.uint8
+FP8X4 = mybir.dt.float8_e4m3fn_x4
+FP4X4 = mybir.dt.float4_e2m1fn_x4
+COPY = mybir.ActivationFunctionType.Copy
+ALU = mybir.AluOpType
+
+P = 128
+PACK = 4
+BANK = 512
+CHUNK = 256
+HALF = I // 2
+LIST_COLS = I // 16
+CAST_ON_SCALAR = 48
+SPLIT = 688
+FIRST = 64
+
+
+def tile_attend_slopes_side_kernel(tc, states, wq_words, wq_scales, cache_words, cache_scales,
+                                    draft_words, draft_scales, offs, offs2, offs3, offs4, out):
+    nc = tc.nc
+    with ExitStack() as ctx:
+        sb = ctx.enter_context(tc.tile_pool(name="sb", bufs=1))
+        psum = ctx.enter_context(tc.psum_pool(name="psum", bufs=1))
+
+        def load_scale_rows(queue, scales, name):
+            width = scales.shape[2] // 4
+            staged = sb.tile([4, 4, width], I32, name=name + "_staged")
+            queue.dma_start(out=staged[:], in_=scales[0].bitcast(I32).rearrange("(g r) n -> r g n", r=4))
+            return staged
+
+        def new_plane(width, name):
+            plane = sb.tile([P, width], U8, name=name, align_bytes=64)
+            nc.vector.memset(plane[:].bitcast(I32), 0)
+            return plane
+
+        def spread_scale_rows(plane, staged):
+            for g in range(4):
+                nc.vector.tensor_copy(out=plane[32 * g : 32 * g + 4, :].bitcast(I32), in_=staged[:, g, :])
+
+        def load_list(src, name):
+            lst = sb.tile([P, LIST_COLS], U16, name=name)
+            nc.sync.dma_start(lst[:], src)
+            return lst
+
+        wq_staged = load_scale_rows(nc.scalar, wq_scales, "wq")
+        raw = sb.tile([P, PACK, Q], F32)
+        nc.sync.dma_start(out=raw[:], in_=states.rearrange("(p j) q -> p j q", j=PACK))
+        wq_nat = sb.tile([P, K], U32, align_bytes=64)
+        nc.sync.dma_start(out=wq_nat[:].bitcast(I32), in_=wq_words[0].rearrange("p n t -> p (n t)").bitcast(I32))
+        cache_staged = load_scale_rows(nc.sync, cache_scales, "cache")
+        cache_w = sb.tile([P, 2 * T], U8, align_bytes=64)
+        nc.sync.dma_start(out=cache_w[:].bitcast(I32), in_=cache_words[0].bitcast(I32))
+        idx = load_list(offs, "idx")
+        draft_staged = load_scale_rows(nc.sync, draft_scales, "draft")
+        draft_w = sb.tile([P, U], U32, align_bytes=64)
+        nc.sync.dma_start(out=draft_w[:].bitcast(I32), in_=draft_words[0].rearrange("p n t -> p (n t)").bitcast(I32))
+        idx2 = load_list(offs2, "idx2")
+        idx4 = load_list(offs4, "idx4")
+        idx3 = load_list(offs3, "idx3")
+
+        wq_nat_s = new_plane(K, "wq_nat_s")
+        cache_s = new_plane(T, "cache_s")
+        draft_s = new_plane(U, "draft_s")
+        a_prev = sb.tile([P, T + 8], F32)
+        nc.vector.memset(a_prev[:, 0:1], 0.0)
+        f1 = sb.tile([P, U], F32)
+        nc.vector.memset(f1[:], 0.0)
+        f2 = sb.tile([P, T], F32)
+        nc.vector.memset(f2[:], 0.0)
+
+        spread_scale_rows(wq_nat_s, wq_staged)
+        wq_s = sb.tile([P, K], U8, align_bytes=64)
+        nc.vector.tensor_copy(out=wq_s[:].rearrange("p (t m) -> p m t", t=PACK),
+                              in_=wq_nat_s[:].rearrange("p (m t) -> p m t", t=PACK))
+
+        st_bf = sb.tile([P, Q, PACK], BF16, align_bytes=64)
+        nc.scalar.activation(st_bf[:, :CAST_ON_SCALAR, :], raw[:, :, :CAST_ON_SCALAR].rearrange("p j q -> p q j"), COPY)
+        nc.vector.tensor_copy(out=st_bf[:, CAST_ON_SCALAR:, :], in_=raw[:, :, CAST_ON_SCALAR:].rearrange("p j q -> p q j"))
+        st_w = sb.tile([P, Q], U32, align_bytes=64)
+        st_s = sb.tile([P, Q], U8, align_bytes=64)
+        nc.vector.quantize_mx(out=st_w[:].bitcast(FP8X4), scales=st_s[:], in_=st_bf[:].rearrange("p q j -> p (q j)"))
+
+        wq_w = sb.tile([P, K], U32, align_bytes=64)
+        dealt = wq_w[:].rearrange("p (t m) -> p m t", t=PACK)
+        natural = wq_nat[:].rearrange("p (m t) -> p m t", t=PACK)
+        nc.scalar.copy(dealt[:, : P // 2, :], natural[:, : P // 2, :])
+        nc.vector.tensor_copy(out=dealt[:, P // 2 :, :], in_=natural[:, P // 2 :, :])
+
+        qv_ps = psum.tile([P, PACK, Q], F32)
+        for t in range(PACK):
+            cols = slice(t * P, (t + 1) * P)
+            nc.tensor.matmul_mx(out=qv_ps[:, t, :], lhsT=wq_w[:, cols].bitcast(FP8X4), lhsT_scale=wq_s[:, cols],
+                                rhs=st_w[:].bitcast(FP8X4), rhs_scale=st_s[:], start=True, stop=True)
+        spread_scale_rows(cache_s, cache_staged)
+        qv_bf = sb.tile([P, Q, PACK], BF16, align_bytes=64)
+        nc.scalar.copy(qv_bf[:], qv_ps[:].rearrange("p t q -> p q t"))
+        qv_w = sb.tile([P, Q], U32, align_bytes=64)
+        qv_s = sb.tile([P, Q], U8, align_bytes=64)
+        nc.vector.quantize_mx(out=qv_w[:].bitcast(FP8X4), scales=qv_s[:], in_=qv_bf[:].rearrange("p q j -> p (q j)"))
+
+        dl = sb.tile([P, T], F32)
+        a_ps = []
+        for c in range(T // CHUNK):
+            lo, hi = c * CHUNK, (c + 1) * CHUNK
+            bank = psum.tile([P, CHUNK], F32, name=f"a_ps{c}")
+            a_ps.append(bank)
+            nc.tensor.matmul_mx(out=bank[:], lhsT=qv_w[:].bitcast(FP8X4), lhsT_scale=qv_s[:],
+                                rhs=cache_w[:, 2 * lo : 2 * hi].bitcast(FP4X4), rhs_scale=cache_s[:, lo:hi],
+                                start=True, stop=True)
+            nc.scalar.copy(a_prev[:, lo + 1 : hi + 1], bank[:])
+            nc.vector.tensor_tensor(dl[:, lo:hi], bank[:], a_prev[:, lo:hi], ALU.subtract)
+
+        halves = [(slice(h * HALF, (h + 1) * HALF), slice(h * LIST_COLS // 2, (h + 1) * LIST_COLS // 2)) for h in range(2)]
+
+        def gather_on_both(dst0, dst1, window, lst):
+            nc.vector.tensor_copy(dst0, window[:].indirect(lst[:, halves[0][1]]))
+            nc.scalar.activation(dst1, window[:].indirect(lst[:, halves[1][1]]), COPY)
+
+        step = sb.tile([P, I], F32)
+        gather_on_both(step[:, :HALF], step[:, HALF:], dl, idx)
+        nc.scalar.activation(f1[:].indirect(idx2[:]), step[:], COPY)
+
+        spread_scale_rows(draft_s, draft_staged)
+        b_ps = []
+        for c in range(U // BANK):
+            cols = slice(c * BANK, (c + 1) * BANK)
+            bank = psum.tile([P, BANK], F32, name=f"b_ps{c}")
+            b_ps.append(bank)
+            nc.tensor.matmul_mx(out=bank[:], lhsT=st_w[:].bitcast(FP8X4), lhsT_scale=st_s[:],
+                                rhs=draft_w[:, cols].bitcast(FP8X4), rhs_scale=draft_s[:, cols], start=True, stop=True)
+
+        step4 = sb.tile([P, I], F32)
+        nc.vector.tensor_copy(step4[:], dl[:].indirect(idx4[:]))
+        b_tail = sb.tile([P, U - SPLIT], F32)
+        nc.vector.tensor_copy(b_tail[:], b_ps[1][:, SPLIT - BANK :])
+
+        bb = sb.tile([P, U], F32)
+        nc.gpsimd.tensor_tensor(bb[:, SPLIT:], b_tail[:], f1[:, SPLIT:], ALU.add)
+        nc.vector.tensor_tensor(bb[:, :BANK], b_ps[0][:], f1[:, :BANK], ALU.add)
+        nc.vector.tensor_tensor(bb[:, BANK:SPLIT], b_ps[1][:, : SPLIT - BANK], f1[:, BANK:SPLIT], ALU.add)
+
+        picked = sb.tile([P, I], F32)
+        v = sb.tile([P, I], F32)
+        gather_on_both(picked[:, :HALF], picked[:, HALF:], bb, idx3)
+        for lo, hi in ((0, FIRST), (FIRST, I)):
+            nc.vector.tensor_tensor(v[:, lo:hi], picked[:, lo:hi], step4[:, lo:hi], ALU.max)
+            nc.scalar.activation(f2[:].indirect(idx[:, lo // 16 : hi // 16]), v[:, lo:hi], COPY)
+
+        aa = sb.tile([P, T], F32)
+        nc.gpsimd.tensor_tensor(aa[:, SPLIT:], a_prev[:, SPLIT + 1 : T + 1], f2[:, SPLIT:], ALU.subtract)
+        for c in range(T // CHUNK):
+            lo, hi = c * CHUNK, min((c + 1) * CHUNK, SPLIT)
+            if lo < hi:
+                nc.vector.tensor_tensor(aa[:, lo:hi], a_ps[c][:, : hi - lo], f2[:, lo:hi], ALU.subtract)
+
+        y0 = sb.tile([P, HALF], F32)
+        y1 = sb.tile([P, HALF], F32)
+        gather_on_both(y0[:], y1[:], aa, idx4)
+        nc.sync.dma_start(out=out[:, :HALF], in_=y0[:])
+        nc.scalar.dma_start(out=out[:, HALF:], in_=y1[:])

@@ -40,8 +40,8 @@ def tile_attend_slopes_side_kernel(tc, states, wq_words, wq_scales, cache_words,
             queue.dma_start(out=staged[:], in_=scales[0].bitcast(I32).rearrange("(g r) n -> r g n", r=4))
             return staged
 
-        def new_plane(width, name):
-            plane = sb.tile([P, width], U8, name=name, align_bytes=64)
+        def new_plane(width, name, tag):
+            plane = sb.tile([P, width], U8, name=name, tag=tag, align_bytes=64)
             nc.vector.memset(plane[:].bitcast(I32), 0)
             return plane
 
@@ -70,9 +70,7 @@ def tile_attend_slopes_side_kernel(tc, states, wq_words, wq_scales, cache_words,
         idx4 = load_list(offs4, "idx4")
         idx3 = load_list(offs3, "idx3")
 
-        wq_nat_s = new_plane(K, "wq_nat_s")
-        cache_s = new_plane(T, "cache_s")
-        draft_s = new_plane(U, "draft_s")
+        wq_nat_s = new_plane(K, "wq_nat_s", "wq_nat_s")
         a_prev = sb.tile([P, T + 8], F32)
         nc.vector.memset(a_prev[:, 0:1], 0.0)
         f1 = sb.tile([P, U], F32)
@@ -82,34 +80,39 @@ def tile_attend_slopes_side_kernel(tc, states, wq_words, wq_scales, cache_words,
 
         spread_scale_rows(wq_nat_s, wq_staged)
         wq_s = sb.tile([P, K], U8, align_bytes=64)
-        nc.vector.tensor_copy(out=wq_s[:].rearrange("p (t m) -> p m t", t=PACK),
-                              in_=wq_nat_s[:].rearrange("p (m t) -> p m t", t=PACK))
+        nc.vector.tensor_copy(out=wq_s[:].rearrange("p (t c i) -> p c t i", t=PACK, i=16),
+                              in_=wq_nat_s[:].rearrange("p (c i t) -> p c t i", t=PACK, i=16))
 
-        st_bf = sb.tile([P, Q, PACK], BF16, align_bytes=64)
-        nc.scalar.activation(st_bf[:, :CAST_ON_SCALAR, :], raw[:, :, :CAST_ON_SCALAR].rearrange("p j q -> p q j"), COPY)
-        nc.vector.tensor_copy(out=st_bf[:, CAST_ON_SCALAR:, :], in_=raw[:, :, CAST_ON_SCALAR:].rearrange("p j q -> p q j"))
+        st_bf = sb.tile([P, Q, PACK], BF16, tag="st_bf", align_bytes=64)
+        woven = st_bf[:].rearrange("p (c i) j -> p c j i", i=4)
+        rows = raw[:].rearrange("p j (c i) -> p c j i", i=4)
+        nc.scalar.activation(woven[:, : CAST_ON_SCALAR // 4], rows[:, : CAST_ON_SCALAR // 4], COPY)
+        nc.vector.tensor_copy(out=woven[:, CAST_ON_SCALAR // 4 :], in_=rows[:, CAST_ON_SCALAR // 4 :])
         st_w = sb.tile([P, Q], U32, align_bytes=64)
         st_s = sb.tile([P, Q], U8, align_bytes=64)
         nc.vector.quantize_mx(out=st_w[:].bitcast(FP8X4), scales=st_s[:], in_=st_bf[:].rearrange("p q j -> p (q j)"))
 
         wq_w = sb.tile([P, K], U32, align_bytes=64)
-        dealt = wq_w[:].rearrange("p (t m) -> p m t", t=PACK)
-        natural = wq_nat[:].rearrange("p (m t) -> p m t", t=PACK)
-        nc.scalar.copy(dealt[:, : P // 2, :], natural[:, : P // 2, :])
-        nc.vector.tensor_copy(out=dealt[:, P // 2 :, :], in_=natural[:, P // 2 :, :])
+        dealt = wq_w[:].rearrange("p (t c i) -> p c t i", t=PACK, i=4)
+        natural = wq_nat[:].rearrange("p (c i t) -> p c t i", t=PACK, i=4)
+        nc.scalar.copy(dealt[:, :16], natural[:, :16])
+        nc.vector.tensor_copy(out=dealt[:, 16:], in_=natural[:, 16:])
 
         qv_ps = psum.tile([P, PACK, Q], F32)
         for t in range(PACK):
             cols = slice(t * P, (t + 1) * P)
             nc.tensor.matmul_mx(out=qv_ps[:, t, :], lhsT=wq_w[:, cols].bitcast(FP8X4), lhsT_scale=wq_s[:, cols],
                                 rhs=st_w[:].bitcast(FP8X4), rhs_scale=st_s[:], start=True, stop=True)
+        cache_s = new_plane(T, "cache_s", "st_bf")
         spread_scale_rows(cache_s, cache_staged)
-        qv_bf = sb.tile([P, Q, PACK], BF16, align_bytes=64)
+        qv_bf = sb.tile([P, Q, PACK], BF16, tag="qv_bf", align_bytes=64)
         nc.scalar.copy(qv_bf[:], qv_ps[:].rearrange("p t q -> p q t"))
         qv_w = sb.tile([P, Q], U32, align_bytes=64)
         qv_s = sb.tile([P, Q], U8, align_bytes=64)
         nc.vector.quantize_mx(out=qv_w[:].bitcast(FP8X4), scales=qv_s[:], in_=qv_bf[:].rearrange("p q j -> p (q j)"))
 
+        draft_s = new_plane(U, "draft_s", "qv_bf")
+        spread_scale_rows(draft_s, draft_staged)
         dl = sb.tile([P, T], F32)
         a_ps = []
         for c in range(T // CHUNK):
@@ -132,7 +135,6 @@ def tile_attend_slopes_side_kernel(tc, states, wq_words, wq_scales, cache_words,
         gather_on_both(step[:, :HALF], step[:, HALF:], dl, idx)
         nc.scalar.activation(f1[:].indirect(idx2[:]), step[:], COPY)
 
-        spread_scale_rows(draft_s, draft_staged)
         b_ps = []
         for c in range(U // BANK):
             cols = slice(c * BANK, (c + 1) * BANK)

@@ -64,7 +64,7 @@ def tile_attend_slopes_side_kernel(tc, states, wq_words, wq_scales, cache_words,
         nc.sync.dma_start(out=cache_w[:].bitcast(I32), in_=cache_words[0].bitcast(I32))
         idx = load_list(offs, "idx")
         draft_staged = load_scale_rows(nc.sync, draft_scales, "draft")
-        draft_w = sb.tile([P, U], U32, align_bytes=64)
+        draft_w = sb.tile([P, U], U32, tag="draft_w", align_bytes=64)
         nc.sync.dma_start(out=draft_w[:].bitcast(I32), in_=draft_words[0].rearrange("p n t -> p (n t)").bitcast(I32))
         idx2 = load_list(offs2, "idx2")
         idx4 = load_list(offs4, "idx4")
@@ -75,8 +75,6 @@ def tile_attend_slopes_side_kernel(tc, states, wq_words, wq_scales, cache_words,
         nc.vector.memset(a_prev[:, 0:1], 0.0)
         f1 = sb.tile([P, U], F32)
         nc.vector.memset(f1[:], 0.0)
-        f2 = sb.tile([P, T], F32)
-        nc.vector.memset(f2[:], 0.0)
 
         spread_scale_rows(wq_nat_s, wq_staged)
         wq_s = sb.tile([P, K], U8, align_bytes=64)
@@ -148,6 +146,11 @@ def tile_attend_slopes_side_kernel(tc, states, wq_words, wq_scales, cache_words,
         b_tail = sb.tile([P, U - SPLIT], F32)
         nc.vector.tensor_copy(b_tail[:], b_ps[1][:, SPLIT - BANK :])
 
+        f2_first = sb.tile([P, T], F32, tag="draft_w", align_bytes=64)
+        nc.vector.memset(f2_first[:], 0.0)
+        f2_rest = sb.tile([P, T], F32, tag="qv_bf", align_bytes=64)
+        nc.vector.memset(f2_rest[:], 0.0)
+
         bb = sb.tile([P, U], F32)
         nc.gpsimd.tensor_tensor(bb[:, SPLIT:], b_tail[:], f1[:, SPLIT:], ALU.add)
         nc.vector.tensor_tensor(bb[:, :BANK], b_ps[0][:], f1[:, :BANK], ALU.add)
@@ -156,16 +159,14 @@ def tile_attend_slopes_side_kernel(tc, states, wq_words, wq_scales, cache_words,
         picked = sb.tile([P, I], F32)
         v = sb.tile([P, I], F32)
         gather_on_both(picked[:, :HALF], picked[:, HALF:], bb, idx3)
-        for lo, hi in ((0, FIRST), (FIRST, I)):
+        for f2, lo, hi in ((f2_first, 0, FIRST), (f2_rest, FIRST, I)):
             nc.vector.tensor_tensor(v[:, lo:hi], picked[:, lo:hi], step4[:, lo:hi], ALU.max)
             nc.scalar.activation(f2[:].indirect(idx[:, lo // 16 : hi // 16]), v[:, lo:hi], COPY)
 
+        a_less_first = sb.tile([P, T], F32)
+        nc.vector.tensor_tensor(a_less_first[:], a_prev[:, 1 : T + 1], f2_first[:], ALU.subtract)
         aa = sb.tile([P, T], F32)
-        nc.gpsimd.tensor_tensor(aa[:, SPLIT:], a_prev[:, SPLIT + 1 : T + 1], f2[:, SPLIT:], ALU.subtract)
-        for c in range(T // CHUNK):
-            lo, hi = c * CHUNK, min((c + 1) * CHUNK, SPLIT)
-            if lo < hi:
-                nc.vector.tensor_tensor(aa[:, lo:hi], a_ps[c][:, : hi - lo], f2[:, lo:hi], ALU.subtract)
+        nc.vector.tensor_tensor(aa[:], a_less_first[:], f2_rest[:], ALU.subtract)
 
         y0 = sb.tile([P, HALF], F32)
         y1 = sb.tile([P, HALF], F32)

@@ -54,29 +54,35 @@ def tile_attend_slopes_side_kernel(tc, states, wq_words, wq_scales, cache_words,
             nc.sync.dma_start(lst[:], src)
             return lst
 
-        wq_staged = load_scale_rows(nc.scalar, wq_scales, "wq")
         raw = sb.tile([P, PACK, Q], F32)
         nc.sync.dma_start(out=raw[:], in_=states.rearrange("(p j) q -> p j q", j=PACK))
+        wq_nat_s = sb.tile([P, K], U8, align_bytes=64)
+        for g in range(4):
+            four_rows = wq_scales[0:1, 4 * g : 4 * g + 4, :].bitcast(I32)
+            queue = nc.scalar if g < 2 else nc.sync
+            queue.dma_start(out=wq_nat_s[32 * g : 32 * (g + 1), :].bitcast(I32), in_=four_rows.to_broadcast([8, 4, K // 4]))
         wq_nat = sb.tile([P, K], U32, align_bytes=64)
         nc.sync.dma_start(out=wq_nat[:].bitcast(I32), in_=wq_words[0].rearrange("p n t -> p (n t)").bitcast(I32))
         cache_staged = load_scale_rows(nc.sync, cache_scales, "cache")
         cache_w = sb.tile([P, 2 * T], U8, align_bytes=64)
         nc.sync.dma_start(out=cache_w[:].bitcast(I32), in_=cache_words[0].bitcast(I32))
         idx = load_list(offs, "idx")
-        draft_staged = load_scale_rows(nc.sync, draft_scales, "draft")
         draft_w = sb.tile([P, U], U32, tag="draft_w", align_bytes=64)
         nc.sync.dma_start(out=draft_w[:].bitcast(I32), in_=draft_words[0].rearrange("p n t -> p (n t)").bitcast(I32))
         idx2 = load_list(offs2, "idx2")
         idx4 = load_list(offs4, "idx4")
         idx3 = load_list(offs3, "idx3")
+        draft_s = new_plane(U, "draft_s", "draft_s")
+        for g in range(4):
+            nc.sync.dma_start(out=draft_s[32 * g : 32 * g + 4, :].bitcast(I32), in_=draft_scales[0, 4 * g : 4 * g + 4, :].bitcast(I32))
 
-        wq_nat_s = new_plane(K, "wq_nat_s", "wq_nat_s")
         a_prev = sb.tile([P, T + 8], F32)
         nc.vector.memset(a_prev[:, 0:1], 0.0)
         f1 = sb.tile([P, U], F32)
-        nc.vector.memset(f1[:], 0.0)
+        nc.gpsimd.memset(f1[:], 0.0)
+        f2 = sb.tile([P, T], F32)
+        nc.vector.memset(f2[:], 0.0)
 
-        spread_scale_rows(wq_nat_s, wq_staged)
         wq_s = sb.tile([P, K], U8, align_bytes=64)
         nc.vector.tensor_copy(out=wq_s[:].rearrange("p (t c i) -> p c t i", t=PACK, i=16),
                               in_=wq_nat_s[:].rearrange("p (c i t) -> p c t i", t=PACK, i=16))
@@ -109,19 +115,21 @@ def tile_attend_slopes_side_kernel(tc, states, wq_words, wq_scales, cache_words,
         qv_s = sb.tile([P, Q], U8, align_bytes=64)
         nc.vector.quantize_mx(out=qv_w[:].bitcast(FP8X4), scales=qv_s[:], in_=qv_bf[:].rearrange("p q j -> p (q j)"))
 
-        draft_s = new_plane(U, "draft_s", "qv_bf")
-        spread_scale_rows(draft_s, draft_staged)
         dl = sb.tile([P, T], F32)
         a_ps = []
-        for c in range(T // CHUNK):
-            lo, hi = c * CHUNK, (c + 1) * CHUNK
-            bank = psum.tile([P, CHUNK], F32, name=f"a_ps{c}")
+        edges = (0, 256, 512, 768, 896, 1024)
+        for c in range(len(edges) - 1):
+            lo, hi = edges[c], edges[c + 1]
+            bank = psum.tile([P, hi - lo], F32, name=f"a_ps{c}", tag=f"bank{c}")
             a_ps.append(bank)
             nc.tensor.matmul_mx(out=bank[:], lhsT=qv_w[:].bitcast(FP8X4), lhsT_scale=qv_s[:],
                                 rhs=cache_w[:, 2 * lo : 2 * hi].bitcast(FP4X4), rhs_scale=cache_s[:, lo:hi],
                                 start=True, stop=True)
             nc.scalar.copy(a_prev[:, lo + 1 : hi + 1], bank[:])
-            nc.vector.tensor_tensor(dl[:, lo:hi], bank[:], a_prev[:, lo:hi], ALU.subtract)
+            if c == 3:
+                nc.gpsimd.tensor_tensor(dl[:, lo:hi], a_prev[:, lo + 1 : hi + 1], a_prev[:, lo:hi], ALU.subtract)
+            else:
+                nc.vector.tensor_tensor(dl[:, lo:hi], bank[:], a_prev[:, lo:hi], ALU.subtract)
 
         halves = [(slice(h * HALF, (h + 1) * HALF), slice(h * LIST_COLS // 2, (h + 1) * LIST_COLS // 2)) for h in range(2)]
 
@@ -133,11 +141,11 @@ def tile_attend_slopes_side_kernel(tc, states, wq_words, wq_scales, cache_words,
         gather_on_both(step[:, :HALF], step[:, HALF:], dl, idx)
         nc.scalar.activation(f1[:].indirect(idx2[:]), step[:], COPY)
 
-        b_ps = []
-        for c in range(U // BANK):
+        b_ps = {}
+        for c in (1, 0):
             cols = slice(c * BANK, (c + 1) * BANK)
-            bank = psum.tile([P, BANK], F32, name=f"b_ps{c}")
-            b_ps.append(bank)
+            bank = psum.tile([P, BANK], F32, name=f"b_ps{c}", tag=f"bank{3 + c}")
+            b_ps[c] = bank
             nc.tensor.matmul_mx(out=bank[:], lhsT=st_w[:].bitcast(FP8X4), lhsT_scale=st_s[:],
                                 rhs=draft_w[:, cols].bitcast(FP8X4), rhs_scale=draft_s[:, cols], start=True, stop=True)
 
@@ -145,11 +153,6 @@ def tile_attend_slopes_side_kernel(tc, states, wq_words, wq_scales, cache_words,
         nc.vector.tensor_copy(step4[:], dl[:].indirect(idx4[:]))
         b_tail = sb.tile([P, U - SPLIT], F32)
         nc.vector.tensor_copy(b_tail[:], b_ps[1][:, SPLIT - BANK :])
-
-        f2_first = sb.tile([P, T], F32, tag="draft_w", align_bytes=64)
-        nc.vector.memset(f2_first[:], 0.0)
-        f2_rest = sb.tile([P, T], F32, tag="qv_bf", align_bytes=64)
-        nc.vector.memset(f2_rest[:], 0.0)
 
         bb = sb.tile([P, U], F32)
         nc.gpsimd.tensor_tensor(bb[:, SPLIT:], b_tail[:], f1[:, SPLIT:], ALU.add)
@@ -159,14 +162,15 @@ def tile_attend_slopes_side_kernel(tc, states, wq_words, wq_scales, cache_words,
         picked = sb.tile([P, I], F32)
         v = sb.tile([P, I], F32)
         gather_on_both(picked[:, :HALF], picked[:, HALF:], bb, idx3)
-        for f2, lo, hi in ((f2_first, 0, FIRST), (f2_rest, FIRST, I)):
+        for lo, hi in ((0, FIRST), (FIRST, I)):
             nc.vector.tensor_tensor(v[:, lo:hi], picked[:, lo:hi], step4[:, lo:hi], ALU.max)
             nc.scalar.activation(f2[:].indirect(idx[:, lo // 16 : hi // 16]), v[:, lo:hi], COPY)
 
-        a_less_first = sb.tile([P, T], F32)
-        nc.vector.tensor_tensor(a_less_first[:], a_prev[:, 1 : T + 1], f2_first[:], ALU.subtract)
         aa = sb.tile([P, T], F32)
-        nc.vector.tensor_tensor(aa[:], a_less_first[:], f2_rest[:], ALU.subtract)
+        nc.gpsimd.tensor_tensor(aa[:, SPLIT:], a_prev[:, SPLIT + 1 : T + 1], f2[:, SPLIT:], ALU.subtract)
+        for c in range(3):
+            lo, hi = edges[c], min(edges[c + 1], SPLIT)
+            nc.vector.tensor_tensor(aa[:, lo:hi], a_ps[c][:, : hi - lo], f2[:, lo:hi], ALU.subtract)
 
         y0 = sb.tile([P, HALF], F32)
         y1 = sb.tile([P, HALF], F32)

@@ -63,9 +63,11 @@ def tile_attend_slopes_side_kernel(tc, states, wq_words, wq_scales, cache_words,
             queue.dma_start(out=wq_nat_s[32 * g : 32 * (g + 1), :].bitcast(I32), in_=four_rows.to_broadcast([8, 4, K // 4]))
         wq_nat = sb.tile([P, K], U32, align_bytes=64)
         nc.sync.dma_start(out=wq_nat[:].bitcast(I32), in_=wq_words[0].rearrange("p n t -> p (n t)").bitcast(I32))
-        cache_staged = load_scale_rows(nc.sync, cache_scales, "cache")
         cache_w = sb.tile([P, 2 * T], U8, align_bytes=64)
         nc.sync.dma_start(out=cache_w[:].bitcast(I32), in_=cache_words[0].bitcast(I32))
+        cache_s = new_plane(T, "cache_s", "cache_s")
+        for g in range(4):
+            nc.sync.dma_start(out=cache_s[32 * g : 32 * g + 4, :].bitcast(I32), in_=cache_scales[0, 4 * g : 4 * g + 4, :].bitcast(I32))
         idx = load_list(offs, "idx")
         draft_w = sb.tile([P, U], U32, tag="draft_w", align_bytes=64)
         nc.sync.dma_start(out=draft_w[:].bitcast(I32), in_=draft_words[0].rearrange("p n t -> p (n t)").bitcast(I32))
@@ -99,16 +101,14 @@ def tile_attend_slopes_side_kernel(tc, states, wq_words, wq_scales, cache_words,
         wq_w = sb.tile([P, K], U32, align_bytes=64)
         dealt = wq_w[:].rearrange("p (t c i) -> p c t i", t=PACK, i=4)
         natural = wq_nat[:].rearrange("p (c i t) -> p c t i", t=PACK, i=4)
-        nc.scalar.copy(dealt[:, :16], natural[:, :16])
-        nc.vector.tensor_copy(out=dealt[:, 16:], in_=natural[:, 16:])
+        nc.scalar.copy(dealt[:, :12], natural[:, :12])
+        nc.vector.tensor_copy(out=dealt[:, 12:], in_=natural[:, 12:])
 
         qv_ps = psum.tile([P, PACK, Q], F32)
         for t in range(PACK):
             cols = slice(t * P, (t + 1) * P)
             nc.tensor.matmul_mx(out=qv_ps[:, t, :], lhsT=wq_w[:, cols].bitcast(FP8X4), lhsT_scale=wq_s[:, cols],
                                 rhs=st_w[:].bitcast(FP8X4), rhs_scale=st_s[:], start=True, stop=True)
-        cache_s = new_plane(T, "cache_s", "st_bf")
-        spread_scale_rows(cache_s, cache_staged)
         qv_bf = sb.tile([P, Q, PACK], BF16, tag="qv_bf", align_bytes=64)
         nc.scalar.copy(qv_bf[:], qv_ps[:].rearrange("p t q -> p q t"))
         qv_w = sb.tile([P, Q], U32, align_bytes=64)

from contextlib import ExitStack

import concourse.mybir as mybir

D, K, T, U, I, Q = 512, 512, 1024, 1024, 512, 128
FLOPS = 2 * (D * K * Q + K * T * Q + D * U * Q)

F32 = mybir.dt.float32
BF16 = mybir.dt.bfloat16
I32 = mybir.dt.int32
U32 = mybir.dt.uint32
U16 = mybir.dt.uint16
U8 = mybir.dt.uint8
FP8X4 = mybir.dt.float8_e4m3fn_x4
FP4X4 = mybir.dt.float4_e2m1fn_x4
COPY = mybir.ActivationFunctionType.Copy
ALU = mybir.AluOpType

P = 128
PACK = 4
BANK = 512
CHUNK = 256
HALF = I // 2
LIST_COLS = I // 16
CAST_ON_SCALAR = 48
SPLIT = 688
FIRST = 64


def tile_attend_slopes_side_kernel(tc, states, wq_words, wq_scales, cache_words, cache_scales,
                                    draft_words, draft_scales, offs, offs2, offs3, offs4, out):
    nc = tc.nc
    with ExitStack() as ctx:
        sb = ctx.enter_context(tc.tile_pool(name="sb", bufs=1))
        psum = ctx.enter_context(tc.psum_pool(name="psum", bufs=1))

        def load_scale_rows(queue, scales, name):
            width = scales.shape[2] // 4
            staged = sb.tile([4, 4, width], I32, name=name + "_staged")
            queue.dma_start(out=staged[:], in_=scales[0].bitcast(I32).rearrange("(g r) n -> r g n", r=4))
            return staged

        def new_plane(width, name, tag):
            plane = sb.tile([P, width], U8, name=name, tag=tag, align_bytes=64)
            nc.vector.memset(plane[:].bitcast(I32), 0)
            return plane

        def spread_scale_rows(plane, staged):
            for g in range(4):
                nc.vector.tensor_copy(out=plane[32 * g : 32 * g + 4, :].bitcast(I32), in_=staged[:, g, :])

        def load_list(src, name):
            lst = sb.tile([P, LIST_COLS], U16, name=name)
            nc.sync.dma_start(lst[:], src)
            return lst

        raw = sb.tile([P, PACK, Q], F32)
        nc.sync.dma_start(out=raw[:], in_=states.rearrange("(p j) q -> p j q", j=PACK))
        wq_nat_s = sb.tile([P, K], U8, align_bytes=64)
        for g in range(4):
            four_rows = wq_scales[0:1, 4 * g : 4 * g + 4, :].bitcast(I32)
            queue = nc.scalar if g < 2 else nc.sync
            queue.dma_start(out=wq_nat_s[32 * g : 32 * (g + 1), :].bitcast(I32), in_=four_rows.to_broadcast([8, 4, K // 4]))
        wq_nat = sb.tile([P, K], U32, align_bytes=64)
        nc.sync.dma_start(out=wq_nat[:].bitcast(I32), in_=wq_words[0].rearrange("p n t -> p (n t)").bitcast(I32))
        cache_w = sb.tile([P, 2 * T], U8, align_bytes=64)
        nc.sync.dma_start(out=cache_w[:].bitcast(I32), in_=cache_words[0].bitcast(I32))
        cache_s = new_plane(T, "cache_s", "cache_s")
        for g in range(4):
            nc.sync.dma_start(out=cache_s[32 * g : 32 * g + 4, :].bitcast(I32), in_=cache_scales[0, 4 * g : 4 * g + 4, :].bitcast(I32))
        idx = load_list(offs, "idx")
        draft_w = sb.tile([P, U], U32, tag="draft_w", align_bytes=64)
        nc.sync.dma_start(out=draft_w[:].bitcast(I32), in_=draft_words[0].rearrange("p n t -> p (n t)").bitcast(I32))
        idx2 = load_list(offs2, "idx2")
        idx4 = load_list(offs4, "idx4")
        idx3 = load_list(offs3, "idx3")
        draft_s = new_plane(U, "draft_s", "draft_s")
        for g in range(4):
            nc.sync.dma_start(out=draft_s[32 * g : 32 * g + 4, :].bitcast(I32), in_=draft_scales[0, 4 * g : 4 * g + 4, :].bitcast(I32))

        a_prev = sb.tile([P, T + 8], F32)
        nc.vector.memset(a_prev[:, 0:1], 0.0)
        f1 = sb.tile([P, U], F32)
        nc.gpsimd.memset(f1[:], 0.0)
        f2 = sb.tile([P, T], F32)
        nc.vector.memset(f2[:], 0.0)

        wq_s = sb.tile([P, K], U8, align_bytes=64)
        nc.vector.tensor_copy(out=wq_s[:].rearrange("p (t c i) -> p c t i", t=PACK, i=16),
                              in_=wq_nat_s[:].rearrange("p (c i t) -> p c t i", t=PACK, i=16))

        st_bf = sb.tile([P, Q, PACK], BF16, tag="st_bf", align_bytes=64)
        woven = st_bf[:].rearrange("p (c i) j -> p c j i", i=4)
        rows = raw[:].rearrange("p j (c i) -> p c j i", i=4)
        nc.scalar.activation(woven[:, : CAST_ON_SCALAR // 4], rows[:, : CAST_ON_SCALAR // 4], COPY)
        nc.vector.tensor_copy(out=woven[:, CAST_ON_SCALAR // 4 :], in_=rows[:, CAST_ON_SCALAR // 4 :])
        st_w = sb.tile([P, Q], U32, align_bytes=64)
        st_s = sb.tile([P, Q], U8, align_bytes=64)
        nc.vector.quantize_mx(out=st_w[:].bitcast(FP8X4), scales=st_s[:], in_=st_bf[:].rearrange("p q j -> p (q j)"))

        wq_w = sb.tile([P, K], U32, align_bytes=64)
        dealt = wq_w[:].rearrange("p (t c i) -> p c t i", t=PACK, i=4)
        natural = wq_nat[:].rearrange("p (c i t) -> p c t i", t=PACK, i=4)
        nc.scalar.copy(dealt[:, :12], natural[:, :12])
        nc.vector.tensor_copy(out=dealt[:, 12:], in_=natural[:, 12:])

        qv_ps = psum.tile([P, PACK, Q], F32)
        for t in range(PACK):
            cols = slice(t * P, (t + 1) * P)
            nc.tensor.matmul_mx(out=qv_ps[:, t, :], lhsT=wq_w[:, cols].bitcast(FP8X4), lhsT_scale=wq_s[:, cols],
                                rhs=st_w[:].bitcast(FP8X4), rhs_scale=st_s[:], start=True, stop=True)
        qv_bf = sb.tile([P, Q, PACK], BF16, tag="qv_bf", align_bytes=64)
        nc.scalar.copy(qv_bf[:], qv_ps[:].rearrange("p t q -> p q t"))
        qv_w = sb.tile([P, Q], U32, align_bytes=64)
        qv_s = sb.tile([P, Q], U8, align_bytes=64)
        nc.vector.quantize_mx(out=qv_w[:].bitcast(FP8X4), scales=qv_s[:], in_=qv_bf[:].rearrange("p q j -> p (q j)"))

        dl = sb.tile([P, T], F32)
        a_ps = []
        edges = (0, 256, 512, 768, 896, 1024)
        for c in range(len(edges) - 1):
            lo, hi = edges[c], edges[c + 1]
            bank = psum.tile([P, hi - lo], F32, name=f"a_ps{c}", tag=f"bank{c}")
            a_ps.append(bank)
            nc.tensor.matmul_mx(out=bank[:], lhsT=qv_w[:].bitcast(FP8X4), lhsT_scale=qv_s[:],
                                rhs=cache_w[:, 2 * lo : 2 * hi].bitcast(FP4X4), rhs_scale=cache_s[:, lo:hi],
                                start=True, stop=True)
            nc.scalar.copy(a_prev[:, lo + 1 : hi + 1], bank[:])
            if c == 3:
                nc.gpsimd.tensor_tensor(dl[:, lo:hi], a_prev[:, lo + 1 : hi + 1], a_prev[:, lo:hi], ALU.subtract)
            else:
                nc.vector.tensor_tensor(dl[:, lo:hi], bank[:], a_prev[:, lo:hi], ALU.subtract)

        halves = [(slice(h * HALF, (h + 1) * HALF), slice(h * LIST_COLS // 2, (h + 1) * LIST_COLS // 2)) for h in range(2)]

        def gather_on_both(dst0, dst1, window, lst):
            nc.vector.tensor_copy(dst0, window[:].indirect(lst[:, halves[0][1]]))
            nc.scalar.activation(dst1, window[:].indirect(lst[:, halves[1][1]]), COPY)

        step = sb.tile([P, I], F32)
        gather_on_both(step[:, :HALF], step[:, HALF:], dl, idx)
        nc.scalar.activation(f1[:].indirect(idx2[:]), step[:], COPY)

        b_ps = {}
        for c in (1, 0):
            cols = slice(c * BANK, (c + 1) * BANK)
            bank = psum.tile([P, BANK], F32, name=f"b_ps{c}", tag=f"bank{3 + c}")
            b_ps[c] = bank
            nc.tensor.matmul_mx(out=bank[:], lhsT=st_w[:].bitcast(FP8X4), lhsT_scale=st_s[:],
                                rhs=draft_w[:, cols].bitcast(FP8X4), rhs_scale=draft_s[:, cols], start=True, stop=True)

        step4 = sb.tile([P, I], F32)
        nc.vector.tensor_copy(step4[:], dl[:].indirect(idx4[:]))
        b_tail = sb.tile([P, U - SPLIT], F32)
        nc.vector.tensor_copy(b_tail[:], b_ps[1][:, SPLIT - BANK :])

        bb = sb.tile([P, U], F32)
        nc.gpsimd.tensor_tensor(bb[:, SPLIT:], b_tail[:], f1[:, SPLIT:], ALU.add)
        nc.vector.tensor_tensor(bb[:, :BANK], b_ps[0][:], f1[:, :BANK], ALU.add)
        nc.vector.tensor_tensor(bb[:, BANK:SPLIT], b_ps[1][:, : SPLIT - BANK], f1[:, BANK:SPLIT], ALU.add)

        picked = sb.tile([P, I], F32)
        v = sb.tile([P, I], F32)
        gather_on_both(picked[:, :HALF], picked[:, HALF:], bb, idx3)
        for lo, hi in ((0, FIRST), (FIRST, I)):
            nc.vector.tensor_tensor(v[:, lo:hi], picked[:, lo:hi], step4[:, lo:hi], ALU.max)
            nc.scalar.activation(f2[:].indirect(idx[:, lo // 16 : hi // 16]), v[:, lo:hi], COPY)

        aa = sb.tile([P, T], F32)
        nc.gpsimd.tensor_tensor(aa[:, SPLIT:], a_prev[:, SPLIT + 1 : T + 1], f2[:, SPLIT:], ALU.subtract)
        for c in range(3):
            lo, hi = edges[c], min(edges[c + 1], SPLIT)
            nc.vector.tensor_tensor(aa[:, lo:hi], a_ps[c][:, : hi - lo], f2[:, lo:hi], ALU.subtract)

        y0 = sb.tile([P, HALF], F32)
        y1 = sb.tile([P, HALF], F32)
        gather_on_both(y0[:], y1[:], aa, idx4)
        nc.sync.dma_start(out=out[:, :HALF], in_=y0[:])
        nc.scalar.dma_start(out=out[:, HALF:], in_=y1[:])
